import numpy as np
import ml_dtypes


def mxq(x, axis, fmt="e4m3"):
    dtype, down = {"e4m3": (ml_dtypes.float8_e4m3fn, 7), "e5m2": (ml_dtypes.float8_e5m2, 14)}[fmt]
    v = np.moveaxis(np.asarray(x, np.float32).astype(ml_dtypes.bfloat16).astype(np.float64), axis, -1)
    blocks = v.reshape(v.shape[:-1] + (-1, 32))
    amax = np.abs(blocks).max(-1, keepdims=True)
    byte = np.maximum(np.where(amax > 0, np.frexp(amax)[1] - 1 + 127, 0) - down, 1)
    scale = np.exp2(byte - 127.0)
    codes = (blocks / scale).astype(np.float32).astype(dtype).astype(np.float64)
    return np.moveaxis((codes * scale).reshape(v.shape), -1, axis)


WIDE = False


def mx_kscale(k):
    if not WIDE:
        return np.ones(k)
    levels = np.array([24, -24, 12, -12, 0])
    if k % 512:
        return np.exp2(np.random.permutation(np.resize(levels, k // 32))).repeat(32)
    a = np.empty((k // 512, 16))
    for p in range(k // 512):
        a[p, :8] = np.random.permutation(np.resize(levels, 8))
        for g in range(8):
            far = levels[np.abs(levels - a[p, g]) >= 10]
            a[p, g + 8] = far[np.random.randint(len(far))]
    return np.exp2(a.ravel()).repeat(32)


def f64(x):
    return np.asarray(x).astype(np.float64)


def striped(idx):
    return np.tile(idx.reshape(-1, 16).T, (8, 1)).astype(np.uint16)


def unstriped(offs):
    return offs[:16].T.reshape(-1).astype(np.int64)


E2M1 = np.array([0.0, 0.5, 1.0, 1.5, 2.0, 3.0, 4.0, 6.0, -0.0, -0.5, -1.0, -1.5, -2.0, -3.0, -4.0, -6.0])


def pack_weight(w, fmt):
    k, n = w.shape
    w = f64(np.asarray(w, np.float32).astype(ml_dtypes.bfloat16)).reshape(k // 32, 32, n)
    amax = np.abs(w).max(1)
    if fmt == "e4m3":
        byte = np.frexp(amax)[1] - 1 + 127 - 7
    else:
        mant, ex = np.frexp(amax / 6.0)
        byte = np.where(mant > 0.5, ex, ex - 1) + 127
    byte = np.clip(np.where(amax > 0, byte, 1), 1, 254)
    scaled = (w * np.exp2(127.0 - byte)[:, None, :]).reshape(k, n).astype(np.float32)
    by_word = np.ascontiguousarray(scaled.reshape(k // 512, 128, 4, n).transpose(0, 1, 3, 2))
    if fmt == "e4m3":
        words = by_word.astype(ml_dtypes.float8_e4m3fn).view(np.uint8)
    else:
        c = by_word.astype(ml_dtypes.float4_e2m1fn).view(np.uint8) & 0xF
        words = (c[..., 0::2] | (c[..., 1::2] << 4)).reshape(k // 512, 128, 2 * n)
    return np.ascontiguousarray(words), np.ascontiguousarray(byte.astype(np.uint8).reshape(k // 512, 16, n))


def unpack_weight(words, scales, fmt):
    g, _, n = scales.shape
    words = np.ascontiguousarray(words).reshape(g, 128, n, -1)
    if fmt == "e4m3":
        vals = words.view(ml_dtypes.float8_e4m3fn).astype(np.float64)
    else:
        nib = np.empty((g, 128, n, 4), np.uint8)
        nib[..., 0::2] = words & 0xF
        nib[..., 1::2] = words >> 4
        vals = E2M1[nib]
    vals = vals * np.repeat(np.exp2(scales.astype(np.float64) - 127.0), 8, axis=1)[..., None]
    return vals.transpose(0, 1, 3, 2).reshape(g * 512, n)


def planes(y):
    n, m = y.shape
    v = y.astype(np.float32).astype(ml_dtypes.bfloat16).astype(np.float64).reshape(n // 32, 32, m)
    top = np.abs(v).max(1)
    byte = np.clip(np.where(top > 0, np.frexp(top)[1] - 1 + 127 - 7, 1), 1, 254)
    codes = (v * np.exp2(127.0 - byte)[:, None, :]).reshape(n, m).astype(np.float32).astype(ml_dtypes.float8_e4m3fn).view(np.uint8)
    words = codes.reshape(n // 512, 128, 4, m).transpose(0, 1, 3, 2)
    return np.ascontiguousarray(words), np.ascontiguousarray(byte.astype(np.uint8).reshape(n // 512, 16, m))


K, R, N, T, J = 512, 1024, 512, 2048, 1024


def setup_inputs():
    n = np.random.standard_normal
    s = mx_kscale(K)[:, None]
    u = mx_kscale(R)[:, None]
    wd = n((R, N)) / np.sqrt(R) / u
    p_tab = pack_weight(n((K, T)) * s, "e4m3")
    p_wu = pack_weight(n((K, R)) / np.sqrt(K) / s * u.T, "e2m1")
    p_wd8 = pack_weight(wd[:512], "e4m3")
    p_wd4 = pack_weight(wd[512:], "e2m1")
    return {
        "tab_words": p_tab[0],
        "tab_scales": p_tab[1],
        "wu_words": p_wu[0],
        "wu_scales": p_wu[1],
        "wd8_words": p_wd8[0],
        "wd8_scales": p_wd8[1],
        "wd4_words": p_wd4[0],
        "wd4_scales": p_wd4[1],
        "rT": (n((N, T))).astype(np.float32),
        "b": (0.3 * n(N)).astype(np.float32),
        "wgo": np.tile(np.random.uniform(0.5, 2.0, J), (128, 1)).astype(np.float32),
        "offs": striped(np.random.permutation(T)[:J]),
    }


def reference(tab_words, tab_scales, wu_words, wu_scales, wd8_words, wd8_scales, wd4_words, wd4_scales, rT, b, wgo, offs):
    idx = unstriped(offs)
    tab_ = unpack_weight(tab_words, tab_scales, "e4m3")[:, idx]
    wu_ = unpack_weight(wu_words, wu_scales, "e2m1")
    a = wu_.T @ tab_
    h = np.maximum(a, 0.0)
    h_ = mxq(h, 0, "e4m3")
    wd8_ = unpack_weight(wd8_words, wd8_scales, "e4m3")
    wd4_ = unpack_weight(wd4_words, wd4_scales, "e2m1")
    y = wd8_.T @ h_[:512] + wd4_.T @ h_[512:]
    out = np.zeros((N, T))
    out[:, idx] = f64(wgo)[0] * (y + f64(rT)[:, idx] + f64(b)[:, None])
    return (out,) + planes(out)

@@ -1,0 +1,250 @@
+from contextlib import ExitStack
+
+import concourse.mybir as mybir
+
+K, R, N, T, J = 512, 1024, 512, 2048, 1024
+FLOPS = 2 * K * R * J + 2 * R * N * J
+
+F32 = mybir.dt.float32
+BF16 = mybir.dt.bfloat16
+I32 = mybir.dt.int32
+U32 = mybir.dt.uint32
+U16 = mybir.dt.uint16
+U8 = mybir.dt.uint8
+FP8X4 = mybir.dt.float8_e4m3fn_x4
+FP4X4 = mybir.dt.float4_e2m1fn_x4
+ACT = mybir.ActivationFunctionType
+ALU = mybir.AluOpType
+
+P = 128
+PACK = 4
+PASS = P * PACK
+LIST_GROUP = 16
+CHUNKS = ((0, 256), (256, 512), (512, 1024))
+OUT_CHUNK = 512
+
+
+def load_scale_rows(queue, plane, rows):
+    for q in range(4):
+        queue.dma_start(out=plane[32 * q : 32 * q + 4, :].bitcast(I32), in_=rows[4 * q : 4 * q + 4, :].bitcast(I32))
+
+
+def tile_list_modp_relu_mix_resbP_kernel(
+    tc, tab_words, tab_scales, wu_words, wu_scales, wd8_words, wd8_scales, wd4_words, wd4_scales, rT, b, wgo, offs,
+    out_0, out_1, out_2,
+):
+    nc = tc.nc
+    with ExitStack() as ctx:
+        lists = ctx.enter_context(tc.tile_pool(name="lists", bufs=1))
+        keep = ctx.enter_context(tc.tile_pool(name="keep", bufs=1))
+        up_banks = ctx.enter_context(tc.psum_pool(name="up_banks", bufs=4))
+        down_banks = ctx.enter_context(tc.psum_pool(name="down_banks", bufs=4))
+
+        offsets = lists.tile([P, J // LIST_GROUP], U16, name="offsets")
+        nc.sync.dma_start(offsets[:], offs)
+
+        def entries(lo, hi):
+            return offsets[:, lo // LIST_GROUP : hi // LIST_GROUP]
+
+        table_scales = keep.tile([P, T], U8, name="table_scales", align_bytes=64)
+        wu_scales_raw = keep.tile([P, R], U8, name="wu_scales_raw", align_bytes=64)
+        wd_scales_raw = keep.tile([P, 2 * N], U8, name="wd_scales_raw", align_bytes=64)
+        nc.vector.memset(wu_scales_raw[:].bitcast(I32), 0)
+        nc.vector.memset(table_scales[:].bitcast(I32), 0)
+        nc.vector.memset(wd_scales_raw[:].bitcast(I32), 0)
+
+        table_words = keep.tile([P, T], U32, name="table_words", tag="table_then_page", align_bytes=64)
+        r_rows = rT.rearrange("(p t) c -> t p c", t=PACK)
+        out_rows = out_0.rearrange("(p t) c -> t p c", t=PACK)
+        wu = keep.tile([P, 2 * R], U8, name="wu", align_bytes=64)
+        wu_sc = keep.tile([P, R], U8, name="wu_sc", align_bytes=64)
+        wd8 = keep.tile([P, N], U32, name="wd8", align_bytes=64)
+        wd4 = keep.tile([P, 2 * N], U8, name="wd4", align_bytes=64)
+        wd_sc = keep.tile([P, 2 * N], U8, name="wd_sc", align_bytes=64)
+
+        def deal(copy, dealt, raw):
+            copy(
+                out=dealt.rearrange("p (g t m) -> p g t m", t=PACK, m=P),
+                in_=raw.rearrange("p (g m t) -> p g t m", t=PACK, m=P),
+            )
+
+        with tc.tile_pool(name="first", bufs=1) as first:
+            wu_raw = first.tile([P, 2 * R], U8, name="wu_raw", align_bytes=64)
+            nc.sync.dma_start(out=wu_raw[:].bitcast(I32), in_=wu_words[0].bitcast(I32))
+            nc.sync.dma_start(out=table_words[:].bitcast(I32), in_=tab_words[0].rearrange("p c i -> p (c i)").bitcast(I32))
+            load_scale_rows(nc.sync, wu_scales_raw, wu_scales[0])
+            load_scale_rows(nc.sync, table_scales, tab_scales[0])
+            deal(nc.scalar.copy, wu[:].bitcast(U16), wu_raw[:].bitcast(U16))
+            deal(nc.vector.tensor_copy, wu_sc[:], wu_scales_raw[:])
+
+        later = ctx.enter_context(tc.tile_pool(name="later", bufs=1))
+        wd8_raw = later.tile([P, N], U32, name="wd8_raw", align_bytes=64)
+        wd4_raw = later.tile([P, 2 * N], U8, name="wd4_raw", align_bytes=64)
+        residual = [later.tile([P, T], F32, name="residual%d" % t, tag="residual%d" % t, align_bytes=64) for t in range(PACK)]
+        bias = later.tile([P, PACK], F32, name="bias", align_bytes=64)
+        weight = later.tile([P, J], F32, name="weight", align_bytes=64)
+        load_scale_rows(nc.sync, wd_scales_raw[:, 0:N], wd8_scales[0])
+        load_scale_rows(nc.sync, wd_scales_raw[:, N : 2 * N], wd4_scales[0])
+        nc.sync.dma_start(out=wd8_raw[:].bitcast(I32), in_=wd8_words[0].rearrange("p c i -> p (c i)").bitcast(I32))
+        nc.sync.dma_start(out=wd4_raw[:].bitcast(I32), in_=wd4_words[0].bitcast(I32))
+        nc.sync.dma_start(out=residual[0][:], in_=r_rows[0])
+        nc.sync.dma_start(out=bias[:], in_=b.rearrange("(p t) -> p t", t=PACK))
+        nc.sync.dma_start(out=weight[:], in_=wgo)
+        for t in range(1, PACK):
+            nc.sync.dma_start(out=residual[t][:], in_=r_rows[t])
+
+        pages = [keep.tile([P, T], F32, name="page%d" % t, align_bytes=64) for t in range(2)]
+        for page in pages:
+            nc.vector.memset(page[:], 0.0)
+
+        picked_words, picked_scales = {}, {}
+
+        def pick_words(c, tag):
+            lo, hi = CHUNKS[c]
+            picked_words[c] = keep.tile([P, hi - lo], U32, name="picked_words%d" % c, tag=tag, align_bytes=64)
+            nc.vector.tensor_copy(picked_words[c][:], table_words[:].indirect(entries(lo, hi)))
+
+        def pick_scales(c, tag):
+            lo, hi = CHUNKS[c]
+            picked_scales[c] = keep.tile([P, hi - lo], U8, name="picked_scales%d" % c, tag=tag, align_bytes=64)
+            nc.vector.tensor_copy(picked_scales[c][:], table_scales[:].indirect(entries(lo, hi)))
+
+        pick_words(0, "words_a")
+        pick_scales(0, "scales_a")
+        pick_words(1, "words_b")
+        pick_scales(1, "scales_b")
+
+        deal(nc.scalar.copy, wd8[:], wd8_raw[:])
+        deal(nc.scalar.copy, wd4[:].bitcast(U16), wd4_raw[:].bitcast(U16))
+        deal(nc.vector.tensor_copy, wd_sc[:], wd_scales_raw[:])
+
+        biased = [keep.tile([P, J], F32, name="biased%d" % t, align_bytes=64) for t in range(PACK)]
+        summed = [keep.tile([P, J], F32, name="summed%d" % t, align_bytes=64) for t in range(PACK)]
+
+        def mlp(c):
+            lo, hi = CHUNKS[c]
+            width = hi - lo
+            h = [keep.tile([P, width * PACK], BF16, name="h%d_%d" % (c, g), tag="h%d_%d" % (c, g), align_bytes=64) for g in range(2)]
+            h_words = keep.tile([P, 2 * width], U32, name="h_words%d" % c, align_bytes=64)
+            h_scales = keep.tile([P, 2 * width], U8, name="h_scales%d" % c, align_bytes=64)
+            for g in range(2):
+                for j0 in range(0, width, P):
+                    bank = up_banks.tile([P, PACK, P], F32, name="up_bank")
+                    for t in range(PACK):
+                        col = PASS * g + P * t
+                        nc.tensor.matmul_mx(
+                            out=bank[:, t, :],
+                            lhsT=wu[:, 2 * col : 2 * (col + P)].bitcast(FP4X4),
+                            lhsT_scale=wu_sc[:, col : col + P],
+                            rhs=picked_words[c][:, j0 : j0 + P].bitcast(FP8X4),
+                            rhs_scale=picked_scales[c][:, j0 : j0 + P],
+                            start=True,
+                            stop=True,
+                        )
+                    nc.scalar.activation(
+                        out=h[g][:, PACK * j0 : PACK * (j0 + P)].rearrange("p (j t) -> p j t", t=PACK),
+                        in_=bank[:].rearrange("p t j -> p j t"),
+                        func=ACT.Relu,
+                    )
+                nc.vector.quantize_mx(
+                    out=h_words[:, g * width : (g + 1) * width].bitcast(FP8X4),
+                    scales=h_scales[:, g * width : (g + 1) * width],
+                    in_=h[g][:],
+                )
+            for t in range(PACK):
+                bank = down_banks.tile([P, 512], F32, name="down_bank")
+                nc.tensor.matmul_mx(
+                    out=bank[:, 0:width],
+                    lhsT=wd8[:, P * t : P * (t + 1)].bitcast(FP8X4),
+                    lhsT_scale=wd_sc[:, P * t : P * (t + 1)],
+                    rhs=h_words[:, 0:width].bitcast(FP8X4),
+                    rhs_scale=h_scales[:, 0:width],
+                    start=True,
+                    stop=False,
+                )
+                nc.tensor.matmul_mx(
+                    out=bank[:, 0:width],
+                    lhsT=wd4[:, 2 * P * t : 2 * P * (t + 1)].bitcast(FP4X4),
+                    lhsT_scale=wd_sc[:, N + P * t : N + P * (t + 1)],
+                    rhs=h_words[:, width : 2 * width].bitcast(FP8X4),
+                    rhs_scale=h_scales[:, width : 2 * width],
+                    start=False,
+                    stop=True,
+                )
+                nc.scalar.activation(
+                    out=biased[t][:, lo:hi], in_=bank[:, 0:width], func=ACT.Identity, bias=bias[:, t : t + 1]
+                )
+
+        def add_residual(t, lo, hi):
+            nc.vector.tensor_tensor(summed[t][:, lo:hi], residual[t][:].indirect(entries(lo, hi)), biased[t][:, lo:hi], ALU.add)
+
+        def place(t, lo, hi):
+            nc.vector.tensor_tensor(pages[t][:].indirect(entries(lo, hi)), summed[t][:, lo:hi], weight[:, lo:hi], ALU.mult)
+
+        n_out = T // OUT_CHUNK
+        on_vector = 2
+        grouped = [keep.tile([P, OUT_CHUNK, PACK], BF16, name="grouped%d" % k, align_bytes=64) for k in range(n_out)]
+        pairs = [keep.tile([P, 2, OUT_CHUNK], BF16, name="pairs%d" % k, align_bytes=64) for k in range(on_vector)]
+        out_words = keep.tile([P, T], U32, name="out_words", align_bytes=64)
+        out_scales = keep.tile([P, T], U8, name="out_scales", align_bytes=64)
+
+        def cols(k):
+            return slice(k * OUT_CHUNK, (k + 1) * OUT_CHUNK)
+
+        def finish(t):
+            nc.sync.dma_start(out=out_rows[t], in_=pages[t][:])
+            if t < PACK - 1:
+                for k in range(n_out):
+                    if t == 2 and k < on_vector:
+                        nc.scalar.copy(out=pairs[k][:, 0, :], in_=pages[t][:, cols(k)])
+                    else:
+                        nc.scalar.copy(out=grouped[k][:, :, t], in_=pages[t][:, cols(k)])
+
+        mlp(0)
+        pick_words(2, "words_a")
+        pick_scales(2, "h0_1")
+        add_residual(0, 0, 256)
+        add_residual(1, 0, 256)
+        place(0, 0, 256)
+        mlp(1)
+        place(1, 0, 256)
+        add_residual(0, 256, 512)
+        mlp(2)
+        place(0, 256, 512)
+        add_residual(0, 512, J)
+        add_residual(1, 256, J)
+        place(0, 512, J)
+        finish(0)
+
+        page2 = keep.tile([P, T], F32, name="page2", tag="table_then_page", align_bytes=64)
+        page3 = later.tile([P, T], F32, name="page3", tag="residual0", align_bytes=64)
+        pages.extend([page2, page3])
+        nc.gpsimd.memset(page2[:], 0.0)
+        nc.gpsimd.memset(page3[:], 0.0)
+
+        add_residual(2, 0, J)
+        place(1, 256, J)
+        finish(1)
+        add_residual(3, 0, J)
+        place(2, 0, J)
+        finish(2)
+        place(3, 0, J)
+        finish(3)
+
+        for k in range(on_vector, n_out):
+            nc.scalar.copy(out=grouped[k][:, :, 3], in_=pages[3][:, cols(k)])
+        for k in range(on_vector):
+            nc.vector.tensor_copy(out=pairs[k][:, 1, :], in_=pages[3][:, cols(k)])
+        for k in range(on_vector):
+            nc.vector.tensor_copy(out=grouped[k][:, :, 2:4], in_=pairs[k][:].rearrange("p e c -> p c e"))
+        words_out = out_1[0].rearrange("p c i -> p (c i)").bitcast(I32)
+        for k in range(n_out):
+            nc.vector.quantize_mx(
+                out=out_words[:, cols(k)].bitcast(FP8X4),
+                scales=out_scales[:, cols(k)],
+                in_=grouped[k][:].rearrange("p c t -> p (c t)"),
+            )
+            nc.sync.dma_start(out=words_out[:, cols(k)], in_=out_words[:, cols(k)].bitcast(I32))
+        for q in range(4):
+            queue = nc.sync if q % 2 else nc.scalar
+            queue.dma_start(out=out_2[0][4 * q : 4 * q + 4, :].bitcast(I32), in_=out_scales[32 * q : 32 * q + 4, :].bitcast(I32))

@@ -21,7 +21,8 @@ PACK = 4
 PASS = P * PACK
 LIST_GROUP = 16
 CHUNKS = ((0, 256), (256, 512), (512, 1024))
-OUT_CHUNK = 512
+OUT_CHUNKS = ((0, 512), (512, 768), (768, 1280), (1280, 1792), (1792, 2048))
+ON_VECTOR = 2
 
 
 def load_scale_rows(queue, plane, rows):
@@ -37,6 +38,7 @@ def tile_list_modp_relu_mix_resbP_kernel(
     with ExitStack() as ctx:
         lists = ctx.enter_context(tc.tile_pool(name="lists", bufs=1))
         keep = ctx.enter_context(tc.tile_pool(name="keep", bufs=1))
+        shared = ctx.enter_context(tc.tile_pool(name="shared", bufs=1))
         up_banks = ctx.enter_context(tc.psum_pool(name="up_banks", bufs=4))
         down_banks = ctx.enter_context(tc.psum_pool(name="down_banks", bufs=4))
 
@@ -47,13 +49,13 @@ def tile_list_modp_relu_mix_resbP_kernel(
             return offsets[:, lo // LIST_GROUP : hi // LIST_GROUP]
 
         table_scales = keep.tile([P, T], U8, name="table_scales", align_bytes=64)
-        wu_scales_raw = keep.tile([P, R], U8, name="wu_scales_raw", align_bytes=64)
+        wu_scales_raw = shared.tile([P, R], U8, name="wu_scales_raw", align_bytes=64, offset=0)
         wd_scales_raw = keep.tile([P, 2 * N], U8, name="wd_scales_raw", align_bytes=64)
-        nc.vector.memset(wu_scales_raw[:].bitcast(I32), 0)
         nc.vector.memset(table_scales[:].bitcast(I32), 0)
+        nc.vector.memset(wu_scales_raw[:].bitcast(I32), 0)
         nc.vector.memset(wd_scales_raw[:].bitcast(I32), 0)
 
-        table_words = keep.tile([P, T], U32, name="table_words", tag="table_then_page", align_bytes=64)
+        table_words = keep.tile([P, T], U32, name="table_words", align_bytes=64)
         r_rows = rT.rearrange("(p t) c -> t p c", t=PACK)
         out_rows = out_0.rearrange("(p t) c -> t p c", t=PACK)
         wu = keep.tile([P, 2 * R], U8, name="wu", align_bytes=64)
@@ -70,12 +72,11 @@ def tile_list_modp_relu_mix_resbP_kernel(
 
         with tc.tile_pool(name="first", bufs=1) as first:
             wu_raw = first.tile([P, 2 * R], U8, name="wu_raw", align_bytes=64)
-            nc.sync.dma_start(out=wu_raw[:].bitcast(I32), in_=wu_words[0].bitcast(I32))
-            nc.sync.dma_start(out=table_words[:].bitcast(I32), in_=tab_words[0].rearrange("p c i -> p (c i)").bitcast(I32))
-            load_scale_rows(nc.sync, wu_scales_raw, wu_scales[0])
+            nc.scalar.dma_start(out=wu_raw[:].bitcast(I32), in_=wu_words[0].bitcast(I32))
+            nc.scalar.dma_start(out=table_words[:].bitcast(I32), in_=tab_words[0].rearrange("p c i -> p (c i)").bitcast(I32))
             load_scale_rows(nc.sync, table_scales, tab_scales[0])
+            load_scale_rows(nc.sync, wu_scales_raw, wu_scales[0])
             deal(nc.scalar.copy, wu[:].bitcast(U16), wu_raw[:].bitcast(U16))
-            deal(nc.vector.tensor_copy, wu_sc[:], wu_scales_raw[:])
 
         later = ctx.enter_context(tc.tile_pool(name="later", bufs=1))
         wd8_raw = later.tile([P, N], U32, name="wd8_raw", align_bytes=64)
@@ -99,20 +100,22 @@ def tile_list_modp_relu_mix_resbP_kernel(
 
         picked_words, picked_scales = {}, {}
 
-        def pick_words(c, tag):
+        def pick_words(c, pool, **place_at):
             lo, hi = CHUNKS[c]
-            picked_words[c] = keep.tile([P, hi - lo], U32, name="picked_words%d" % c, tag=tag, align_bytes=64)
+            picked_words[c] = pool.tile([P, hi - lo], U32, name="picked_words%d" % c, align_bytes=64, **place_at)
             nc.vector.tensor_copy(picked_words[c][:], table_words[:].indirect(entries(lo, hi)))
 
-        def pick_scales(c, tag):
+        def pick_scales(c, pool, **place_at):
             lo, hi = CHUNKS[c]
-            picked_scales[c] = keep.tile([P, hi - lo], U8, name="picked_scales%d" % c, tag=tag, align_bytes=64)
+            picked_scales[c] = pool.tile([P, hi - lo], U8, name="picked_scales%d" % c, align_bytes=64, **place_at)
             nc.vector.tensor_copy(picked_scales[c][:], table_scales[:].indirect(entries(lo, hi)))
 
-        pick_words(0, "words_a")
-        pick_scales(0, "scales_a")
-        pick_words(1, "words_b")
-        pick_scales(1, "scales_b")
+        pick_scales(0, keep)
+        pick_words(0, keep)
+        pick_scales(1, keep)
+        deal(nc.vector.tensor_copy, wu_sc[:], wu_scales_raw[:])
+        pick_words(1, shared, offset=512)
+        pick_scales(2, shared, offset=0)
 
         deal(nc.scalar.copy, wd8[:], wd8_raw[:])
         deal(nc.scalar.copy, wd4[:].bitcast(U16), wd4_raw[:].bitcast(U16))
@@ -181,15 +184,16 @@ def tile_list_modp_relu_mix_resbP_kernel(
         def place(t, lo, hi):
             nc.vector.tensor_tensor(pages[t][:].indirect(entries(lo, hi)), summed[t][:, lo:hi], weight[:, lo:hi], ALU.mult)
 
-        n_out = T // OUT_CHUNK
-        on_vector = 2
-        grouped = [keep.tile([P, OUT_CHUNK, PACK], BF16, name="grouped%d" % k, align_bytes=64) for k in range(n_out)]
-        pairs = [keep.tile([P, 2, OUT_CHUNK], BF16, name="pairs%d" % k, align_bytes=64) for k in range(on_vector)]
+        n_out = len(OUT_CHUNKS)
+        on_vector = ON_VECTOR
+        widths = [hi - lo for lo, hi in OUT_CHUNKS]
+        grouped = [keep.tile([P, widths[k], PACK], BF16, name="grouped%d" % k, align_bytes=64) for k in range(n_out)]
+        pairs = [keep.tile([P, 2, widths[k]], BF16, name="pairs%d" % k, align_bytes=64) for k in range(on_vector)]
         out_words = keep.tile([P, T], U32, name="out_words", align_bytes=64)
         out_scales = keep.tile([P, T], U8, name="out_scales", align_bytes=64)
 
         def cols(k):
-            return slice(k * OUT_CHUNK, (k + 1) * OUT_CHUNK)
+            return slice(*OUT_CHUNKS[k])
 
         def finish(t):
             nc.sync.dma_start(out=out_rows[t], in_=pages[t][:])
@@ -201,14 +205,13 @@ def tile_list_modp_relu_mix_resbP_kernel(
                         nc.scalar.copy(out=grouped[k][:, :, t], in_=pages[t][:, cols(k)])
 
         mlp(0)
-        pick_words(2, "words_a")
-        pick_scales(2, "h0_1")
+        pick_words(2, keep, tag="h0_1")
         add_residual(0, 0, 256)
-        add_residual(1, 0, 256)
-        place(0, 0, 256)
         mlp(1)
-        place(1, 0, 256)
+        place(0, 0, 256)
+        add_residual(1, 0, 256)
         add_residual(0, 256, 512)
+        place(1, 0, 256)
         mlp(2)
         place(0, 256, 512)
         add_residual(0, 512, J)
@@ -216,8 +219,8 @@ def tile_list_modp_relu_mix_resbP_kernel(
         place(0, 512, J)
         finish(0)
 
-        page2 = keep.tile([P, T], F32, name="page2", tag="table_then_page", align_bytes=64)
-        page3 = later.tile([P, T], F32, name="page3", tag="residual0", align_bytes=64)
+        page2 = later.tile([P, T], F32, name="page2", tag="residual0", align_bytes=64)
+        page3 = later.tile([P, T], F32, name="page3", tag="residual1", align_bytes=64)
         pages.extend([page2, page3])
         nc.gpsimd.memset(page2[:], 0.0)
         nc.gpsimd.memset(page3[:], 0.0)
@@ -238,7 +241,7 @@ def tile_list_modp_relu_mix_resbP_kernel(
         for k in range(on_vector):
             nc.vector.tensor_copy(out=grouped[k][:, :, 2:4], in_=pairs[k][:].rearrange("p e c -> p c e"))
         words_out = out_1[0].rearrange("p c i -> p (c i)").bitcast(I32)
-        for k in range(n_out):
+        for k in (0, 2, 1, 3, 4):
             nc.vector.quantize_mx(
                 out=out_words[:, cols(k)].bitcast(FP8X4),
                 scales=out_scales[:, cols(k)],

@@ -26,8 +26,10 @@ ON_VECTOR = 2
 
 
 def load_scale_rows(queue, plane, rows):
+    width = rows.shape[1] // 4
     for q in range(4):
-        queue.dma_start(out=plane[32 * q : 32 * q + 4, :].bitcast(I32), in_=rows[4 * q : 4 * q + 4, :].bitcast(I32))
+        four_rows = rows.bitcast(I32)[4 * q : 4 * q + 4, :]
+        queue.dma_start(out=plane.bitcast(I32)[32 * q : 32 * q + 32, :], in_=four_rows.unsqueeze(0).to_broadcast([8, 4, width]))
 
 
 def tile_list_modp_relu_mix_resbP_kernel(
@@ -38,7 +40,6 @@ def tile_list_modp_relu_mix_resbP_kernel(
     with ExitStack() as ctx:
         lists = ctx.enter_context(tc.tile_pool(name="lists", bufs=1))
         keep = ctx.enter_context(tc.tile_pool(name="keep", bufs=1))
-        shared = ctx.enter_context(tc.tile_pool(name="shared", bufs=1))
         up_banks = ctx.enter_context(tc.psum_pool(name="up_banks", bufs=4))
         down_banks = ctx.enter_context(tc.psum_pool(name="down_banks", bufs=4))
 
@@ -49,11 +50,8 @@ def tile_list_modp_relu_mix_resbP_kernel(
             return offsets[:, lo // LIST_GROUP : hi // LIST_GROUP]
 
         table_scales = keep.tile([P, T], U8, name="table_scales", align_bytes=64)
-        wu_scales_raw = shared.tile([P, R], U8, name="wu_scales_raw", align_bytes=64, offset=0)
+        wu_scales_raw = keep.tile([P, R], U8, name="wu_scales_raw", align_bytes=64, tag="wu_scales_raw")
         wd_scales_raw = keep.tile([P, 2 * N], U8, name="wd_scales_raw", align_bytes=64)
-        nc.vector.memset(table_scales[:].bitcast(I32), 0)
-        nc.vector.memset(wu_scales_raw[:].bitcast(I32), 0)
-        nc.vector.memset(wd_scales_raw[:].bitcast(I32), 0)
 
         table_words = keep.tile([P, T], U32, name="table_words", align_bytes=64)
         r_rows = rT.rearrange("(p t) c -> t p c", t=PACK)
@@ -70,26 +68,23 @@ def tile_list_modp_relu_mix_resbP_kernel(
                 in_=raw.rearrange("p (g m t) -> p g t m", t=PACK, m=P),
             )
 
-        with tc.tile_pool(name="first", bufs=1) as first:
-            wu_raw = first.tile([P, 2 * R], U8, name="wu_raw", align_bytes=64)
-            nc.scalar.dma_start(out=wu_raw[:].bitcast(I32), in_=wu_words[0].bitcast(I32))
-            nc.scalar.dma_start(out=table_words[:].bitcast(I32), in_=tab_words[0].rearrange("p c i -> p (c i)").bitcast(I32))
-            load_scale_rows(nc.sync, table_scales, tab_scales[0])
-            load_scale_rows(nc.sync, wu_scales_raw, wu_scales[0])
-            deal(nc.scalar.copy, wu[:].bitcast(U16), wu_raw[:].bitcast(U16))
+        wu_raw = keep.tile([P, 2 * R], U8, name="wu_raw", align_bytes=64)
+        wd8_raw = keep.tile([P, N], U32, name="wd8_raw", align_bytes=64)
+        wd4_raw = keep.tile([P, 2 * N], U8, name="wd4_raw", align_bytes=64)
+        residual = [keep.tile([P, T], F32, name="residual%d" % t, tag="residual%d" % t, align_bytes=64) for t in range(PACK)]
+        bias = keep.tile([P, PACK], F32, name="bias", align_bytes=64)
+        weight = keep.tile([P, J], F32, name="weight", align_bytes=64)
 
-        later = ctx.enter_context(tc.tile_pool(name="later", bufs=1))
-        wd8_raw = later.tile([P, N], U32, name="wd8_raw", align_bytes=64)
-        wd4_raw = later.tile([P, 2 * N], U8, name="wd4_raw", align_bytes=64)
-        residual = [later.tile([P, T], F32, name="residual%d" % t, tag="residual%d" % t, align_bytes=64) for t in range(PACK)]
-        bias = later.tile([P, PACK], F32, name="bias", align_bytes=64)
-        weight = later.tile([P, J], F32, name="weight", align_bytes=64)
-        load_scale_rows(nc.sync, wd_scales_raw[:, 0:N], wd8_scales[0])
-        load_scale_rows(nc.sync, wd_scales_raw[:, N : 2 * N], wd4_scales[0])
+        load_scale_rows(nc.sync, table_scales[:], tab_scales[0])
+        nc.sync.dma_start(out=table_words[:].bitcast(I32), in_=tab_words[0].rearrange("p c i -> p (c i)").bitcast(I32))
+        nc.sync.dma_start(out=wu_raw[:].bitcast(I32), in_=wu_words[0].bitcast(I32))
+        load_scale_rows(nc.sync, wu_scales_raw[:], wu_scales[0])
         nc.sync.dma_start(out=wd8_raw[:].bitcast(I32), in_=wd8_words[0].rearrange("p c i -> p (c i)").bitcast(I32))
         nc.sync.dma_start(out=wd4_raw[:].bitcast(I32), in_=wd4_words[0].bitcast(I32))
+        load_scale_rows(nc.sync, wd_scales_raw[:, 0:N], wd8_scales[0])
+        load_scale_rows(nc.gpsimd, wd_scales_raw[:, N : 2 * N], wd4_scales[0])
         nc.sync.dma_start(out=residual[0][:], in_=r_rows[0])
-        nc.sync.dma_start(out=bias[:], in_=b.rearrange("(p t) -> p t", t=PACK))
+        nc.gpsimd.dma_start(out=bias[:], in_=b.rearrange("(p t) -> p t", t=PACK))
         nc.sync.dma_start(out=weight[:], in_=wgo)
         for t in range(1, PACK):
             nc.sync.dma_start(out=residual[t][:], in_=r_rows[t])
@@ -98,38 +93,34 @@ def tile_list_modp_relu_mix_resbP_kernel(
         for page in pages:
             nc.vector.memset(page[:], 0.0)
 
-        picked_words, picked_scales = {}, {}
+        picked_words = {}
 
         def pick_words(c, pool, **place_at):
             lo, hi = CHUNKS[c]
             picked_words[c] = pool.tile([P, hi - lo], U32, name="picked_words%d" % c, align_bytes=64, **place_at)
             nc.vector.tensor_copy(picked_words[c][:], table_words[:].indirect(entries(lo, hi)))
 
-        def pick_scales(c, pool, **place_at):
-            lo, hi = CHUNKS[c]
-            picked_scales[c] = pool.tile([P, hi - lo], U8, name="picked_scales%d" % c, align_bytes=64, **place_at)
-            nc.vector.tensor_copy(picked_scales[c][:], table_scales[:].indirect(entries(lo, hi)))
-
-        pick_scales(0, keep)
+        picked_scales = keep.tile([P, J], U8, name="picked_scales", align_bytes=64)
+        nc.vector.tensor_copy(picked_scales[:], table_scales[:].indirect(offsets[:]))
         pick_words(0, keep)
-        pick_scales(1, keep)
+        for g in range(2):
+            half = slice(g * PASS, (g + 1) * PASS)
+            deal(nc.scalar.copy, wu[:].bitcast(U16)[:, half], wu_raw[:].bitcast(U16)[:, half])
         deal(nc.vector.tensor_copy, wu_sc[:], wu_scales_raw[:])
-        pick_words(1, shared, offset=512)
-        pick_scales(2, shared, offset=0)
-
-        deal(nc.scalar.copy, wd8[:], wd8_raw[:])
-        deal(nc.scalar.copy, wd4[:].bitcast(U16), wd4_raw[:].bitcast(U16))
+        pick_words(1, keep, tag="wu_scales_raw")
+        deal(nc.vector.tensor_copy, wd8[:], wd8_raw[:])
+        deal(nc.vector.tensor_copy, wd4[:].bitcast(U16), wd4_raw[:].bitcast(U16))
         deal(nc.vector.tensor_copy, wd_sc[:], wd_scales_raw[:])
 
-        biased = [keep.tile([P, J], F32, name="biased%d" % t, align_bytes=64) for t in range(PACK)]
-        summed = [keep.tile([P, J], F32, name="summed%d" % t, align_bytes=64) for t in range(PACK)]
+        biased = {}
+        h_words, h_scales, summed = {}, {}, {}
 
-        def mlp(c):
+        def up(c, tag=""):
             lo, hi = CHUNKS[c]
             width = hi - lo
             h = [keep.tile([P, width * PACK], BF16, name="h%d_%d" % (c, g), tag="h%d_%d" % (c, g), align_bytes=64) for g in range(2)]
-            h_words = keep.tile([P, 2 * width], U32, name="h_words%d" % c, align_bytes=64)
-            h_scales = keep.tile([P, 2 * width], U8, name="h_scales%d" % c, align_bytes=64)
+            h_words[c] = keep.tile([P, 2 * width], U32, name="h_words%d" % c, tag=tag, align_bytes=64)
+            h_scales[c] = keep.tile([P, 2 * width], U8, name="h_scales%d" % c, align_bytes=64)
             for g in range(2):
                 for j0 in range(0, width, P):
                     bank = up_banks.tile([P, PACK, P], F32, name="up_bank")
@@ -140,7 +131,7 @@ def tile_list_modp_relu_mix_resbP_kernel(
                             lhsT=wu[:, 2 * col : 2 * (col + P)].bitcast(FP4X4),
                             lhsT_scale=wu_sc[:, col : col + P],
                             rhs=picked_words[c][:, j0 : j0 + P].bitcast(FP8X4),
-                            rhs_scale=picked_scales[c][:, j0 : j0 + P],
+                            rhs_scale=picked_scales[:, lo + j0 : lo + j0 + P],
                             start=True,
                             stop=True,
                         )
@@ -150,18 +141,22 @@ def tile_list_modp_relu_mix_resbP_kernel(
                         func=ACT.Relu,
                     )
                 nc.vector.quantize_mx(
-                    out=h_words[:, g * width : (g + 1) * width].bitcast(FP8X4),
-                    scales=h_scales[:, g * width : (g + 1) * width],
+                    out=h_words[c][:, g * width : (g + 1) * width].bitcast(FP8X4),
+                    scales=h_scales[c][:, g * width : (g + 1) * width],
                     in_=h[g][:],
                 )
-            for t in range(PACK):
+
+        def down(c, slots):
+            lo, hi = CHUNKS[c]
+            width = hi - lo
+            for t in slots:
                 bank = down_banks.tile([P, 512], F32, name="down_bank")
                 nc.tensor.matmul_mx(
                     out=bank[:, 0:width],
                     lhsT=wd8[:, P * t : P * (t + 1)].bitcast(FP8X4),
                     lhsT_scale=wd_sc[:, P * t : P * (t + 1)],
-                    rhs=h_words[:, 0:width].bitcast(FP8X4),
-                    rhs_scale=h_scales[:, 0:width],
+                    rhs=h_words[c][:, 0:width].bitcast(FP8X4),
+                    rhs_scale=h_scales[c][:, 0:width],
                     start=True,
                     stop=False,
                 )
@@ -169,20 +164,25 @@ def tile_list_modp_relu_mix_resbP_kernel(
                     out=bank[:, 0:width],
                     lhsT=wd4[:, 2 * P * t : 2 * P * (t + 1)].bitcast(FP4X4),
                     lhsT_scale=wd_sc[:, N + P * t : N + P * (t + 1)],
-                    rhs=h_words[:, width : 2 * width].bitcast(FP8X4),
-                    rhs_scale=h_scales[:, width : 2 * width],
+                    rhs=h_words[c][:, width : 2 * width].bitcast(FP8X4),
+                    rhs_scale=h_scales[c][:, width : 2 * width],
                     start=False,
                     stop=True,
                 )
+                if t < 2:
+                    biased[t, lo] = keep.tile([P, width], F32, name="biased%d_%d" % (t, c), tag="biased%d_%d" % (t, c), align_bytes=64)[:]
+                elif c == 0:
+                    biased[t, lo] = keep.tile([P, J], F32, name="biased%d" % t, align_bytes=64)[:]
                 nc.scalar.activation(
-                    out=biased[t][:, lo:hi], in_=bank[:, 0:width], func=ACT.Identity, bias=bias[:, t : t + 1]
+                    out=biased[t, lo] if t < 2 else biased[t, 0][:, lo:hi], in_=bank[:, 0:width], func=ACT.Identity, bias=bias[:, t : t + 1]
                 )
 
-        def add_residual(t, lo, hi):
-            nc.vector.tensor_tensor(summed[t][:, lo:hi], residual[t][:].indirect(entries(lo, hi)), biased[t][:, lo:hi], ALU.add)
+        def add_residual(t, lo, hi, tag=""):
+            summed[t, lo] = keep.tile([P, hi - lo], F32, name="summed%d_%d" % (t, lo), tag=tag, align_bytes=64)
+            nc.vector.tensor_tensor(summed[t, lo][:], residual[t][:].indirect(entries(lo, hi)), biased[t, lo], ALU.add)
 
         def place(t, lo, hi):
-            nc.vector.tensor_tensor(pages[t][:].indirect(entries(lo, hi)), summed[t][:, lo:hi], weight[:, lo:hi], ALU.mult)
+            nc.vector.tensor_tensor(pages[t][:].indirect(entries(lo, hi)), summed[t, lo][:], weight[:, lo:hi], ALU.mult)
 
         n_out = len(OUT_CHUNKS)
         on_vector = ON_VECTOR
@@ -204,29 +204,36 @@ def tile_list_modp_relu_mix_resbP_kernel(
                     else:
                         nc.scalar.copy(out=grouped[k][:, :, t], in_=pages[t][:, cols(k)])
 
-        mlp(0)
+        up(0)
+        down(0, (0, 1))
         pick_words(2, keep, tag="h0_1")
         add_residual(0, 0, 256)
-        mlp(1)
         place(0, 0, 256)
-        add_residual(1, 0, 256)
-        add_residual(0, 256, 512)
+        up(1, "biased0_0")
+        down(1, (0, 1))
+        add_residual(1, 0, 256, tag="h1_1")
         place(1, 0, 256)
-        mlp(2)
+        add_residual(0, 256, 512)
         place(0, 256, 512)
+        up(2, "biased0_1")
+        down(2, (0, 1))
+        add_residual(1, 256, 512, tag="h2_1")
+        place(1, 256, 512)
         add_residual(0, 512, J)
-        add_residual(1, 256, J)
+        add_residual(1, 512, J)
+        for c in range(len(CHUNKS)):
+            down(c, (2, 3))
         place(0, 512, J)
         finish(0)
 
-        page2 = later.tile([P, T], F32, name="page2", tag="residual0", align_bytes=64)
-        page3 = later.tile([P, T], F32, name="page3", tag="residual1", align_bytes=64)
+        page2 = keep.tile([P, T], F32, name="page2", tag="residual0", align_bytes=64)
+        page3 = keep.tile([P, T], F32, name="page3", tag="residual1", align_bytes=64)
         pages.extend([page2, page3])
         nc.gpsimd.memset(page2[:], 0.0)
         nc.gpsimd.memset(page3[:], 0.0)
 
         add_residual(2, 0, J)
-        place(1, 256, J)
+        place(1, 512, J)
         finish(1)
         add_residual(3, 0, J)
         place(2, 0, J)
@@ -241,13 +248,17 @@ def tile_list_modp_relu_mix_resbP_kernel(
         for k in range(on_vector):
             nc.vector.tensor_copy(out=grouped[k][:, :, 2:4], in_=pairs[k][:].rearrange("p e c -> p c e"))
         words_out = out_1[0].rearrange("p c i -> p (c i)").bitcast(I32)
-        for k in (0, 2, 1, 3, 4):
+        stored = 0
+        for k in range(n_out):
             nc.vector.quantize_mx(
                 out=out_words[:, cols(k)].bitcast(FP8X4),
                 scales=out_scales[:, cols(k)],
                 in_=grouped[k][:].rearrange("p c t -> p (c t)"),
             )
-            nc.sync.dma_start(out=words_out[:, cols(k)], in_=out_words[:, cols(k)].bitcast(I32))
+            if k >= ON_VECTOR:
+                done = slice(stored, OUT_CHUNKS[k][1])
+                stored = OUT_CHUNKS[k][1]
+                nc.sync.dma_start(out=words_out[:, done], in_=out_words[:, done].bitcast(I32))
         for q in range(4):
             queue = nc.sync if q % 2 else nc.scalar
             queue.dma_start(out=out_2[0][4 * q : 4 * q + 4, :].bitcast(I32), in_=out_scales[32 * q : 32 * q + 4, :].bitcast(I32))

from contextlib import ExitStack

import concourse.mybir as mybir

K, R, N, T, J = 512, 1024, 512, 2048, 1024
FLOPS = 2 * K * R * J + 2 * R * N * J

F32 = mybir.dt.float32
BF16 = mybir.dt.bfloat16
I32 = mybir.dt.int32
U32 = mybir.dt.uint32
U16 = mybir.dt.uint16
U8 = mybir.dt.uint8
FP8X4 = mybir.dt.float8_e4m3fn_x4
FP4X4 = mybir.dt.float4_e2m1fn_x4
ACT = mybir.ActivationFunctionType
ALU = mybir.AluOpType

P = 128
PACK = 4
PASS = P * PACK
LIST_GROUP = 16
CHUNKS = ((0, 256), (256, 512), (512, 1024))
OUT_CHUNKS = ((0, 512), (512, 768), (768, 1280), (1280, 1792), (1792, 2048))
ON_VECTOR = 2


def load_scale_rows(queue, plane, rows):
    width = rows.shape[1] // 4
    for q in range(4):
        four_rows = rows.bitcast(I32)[4 * q : 4 * q + 4, :]
        queue.dma_start(out=plane.bitcast(I32)[32 * q : 32 * q + 32, :], in_=four_rows.unsqueeze(0).to_broadcast([8, 4, width]))


def tile_list_modp_relu_mix_resbP_kernel(
    tc, tab_words, tab_scales, wu_words, wu_scales, wd8_words, wd8_scales, wd4_words, wd4_scales, rT, b, wgo, offs,
    out_0, out_1, out_2,
):
    nc = tc.nc
    with ExitStack() as ctx:
        lists = ctx.enter_context(tc.tile_pool(name="lists", bufs=1))
        keep = ctx.enter_context(tc.tile_pool(name="keep", bufs=1))
        up_banks = ctx.enter_context(tc.psum_pool(name="up_banks", bufs=4))
        down_banks = ctx.enter_context(tc.psum_pool(name="down_banks", bufs=4))

        offsets = lists.tile([P, J // LIST_GROUP], U16, name="offsets")
        nc.sync.dma_start(offsets[:], offs)

        def entries(lo, hi):
            return offsets[:, lo // LIST_GROUP : hi // LIST_GROUP]

        table_scales = keep.tile([P, T], U8, name="table_scales", align_bytes=64)
        wu_scales_raw = keep.tile([P, R], U8, name="wu_scales_raw", align_bytes=64, tag="wu_scales_raw")
        wd_scales_raw = keep.tile([P, 2 * N], U8, name="wd_scales_raw", align_bytes=64)

        table_words = keep.tile([P, T], U32, name="table_words", align_bytes=64)
        r_rows = rT.rearrange("(p t) c -> t p c", t=PACK)
        out_rows = out_0.rearrange("(p t) c -> t p c", t=PACK)
        wu = keep.tile([P, 2 * R], U8, name="wu", align_bytes=64)
        wu_sc = keep.tile([P, R], U8, name="wu_sc", align_bytes=64)
        wd8 = keep.tile([P, N], U32, name="wd8", align_bytes=64)
        wd4 = keep.tile([P, 2 * N], U8, name="wd4", align_bytes=64)
        wd_sc = keep.tile([P, 2 * N], U8, name="wd_sc", align_bytes=64)

        def deal(copy, dealt, raw):
            copy(
                out=dealt.rearrange("p (g t m) -> p g t m", t=PACK, m=P),
                in_=raw.rearrange("p (g m t) -> p g t m", t=PACK, m=P),
            )

        wu_raw = keep.tile([P, 2 * R], U8, name="wu_raw", align_bytes=64)
        wd8_raw = keep.tile([P, N], U32, name="wd8_raw", align_bytes=64)
        wd4_raw = keep.tile([P, 2 * N], U8, name="wd4_raw", align_bytes=64)
        residual = [keep.tile([P, T], F32, name="residual%d" % t, tag="residual%d" % t, align_bytes=64) for t in range(PACK)]
        bias = keep.tile([P, PACK], F32, name="bias", align_bytes=64)
        weight = keep.tile([P, J], F32, name="weight", align_bytes=64)

        load_scale_rows(nc.sync, table_scales[:], tab_scales[0])
        nc.sync.dma_start(out=table_words[:].bitcast(I32), in_=tab_words[0].rearrange("p c i -> p (c i)").bitcast(I32))
        nc.sync.dma_start(out=wu_raw[:].bitcast(I32), in_=wu_words[0].bitcast(I32))
        load_scale_rows(nc.sync, wu_scales_raw[:], wu_scales[0])
        nc.sync.dma_start(out=wd8_raw[:].bitcast(I32), in_=wd8_words[0].rearrange("p c i -> p (c i)").bitcast(I32))
        nc.sync.dma_start(out=wd4_raw[:].bitcast(I32), in_=wd4_words[0].bitcast(I32))
        load_scale_rows(nc.sync, wd_scales_raw[:, 0:N], wd8_scales[0])
        load_scale_rows(nc.gpsimd, wd_scales_raw[:, N : 2 * N], wd4_scales[0])
        nc.sync.dma_start(out=residual[0][:], in_=r_rows[0])
        nc.gpsimd.dma_start(out=bias[:], in_=b.rearrange("(p t) -> p t", t=PACK))
        nc.sync.dma_start(out=weight[:], in_=wgo)
        for t in range(1, PACK):
            nc.sync.dma_start(out=residual[t][:], in_=r_rows[t])

        pages = [keep.tile([P, T], F32, name="page%d" % t, align_bytes=64) for t in range(2)]
        for page in pages:
            nc.vector.memset(page[:], 0.0)

        picked_words = {}

        def pick_words(c, pool, **place_at):
            lo, hi = CHUNKS[c]
            picked_words[c] = pool.tile([P, hi - lo], U32, name="picked_words%d" % c, align_bytes=64, **place_at)
            nc.vector.tensor_copy(picked_words[c][:], table_words[:].indirect(entries(lo, hi)))

        picked_scales = keep.tile([P, J], U8, name="picked_scales", align_bytes=64)
        nc.vector.tensor_copy(picked_scales[:], table_scales[:].indirect(offsets[:]))
        pick_words(0, keep)
        for g in range(2):
            half = slice(g * PASS, (g + 1) * PASS)
            deal(nc.scalar.copy, wu[:].bitcast(U16)[:, half], wu_raw[:].bitcast(U16)[:, half])
        deal(nc.vector.tensor_copy, wu_sc[:], wu_scales_raw[:])
        pick_words(1, keep, tag="wu_scales_raw")
        deal(nc.vector.tensor_copy, wd8[:], wd8_raw[:])
        deal(nc.vector.tensor_copy, wd4[:].bitcast(U16), wd4_raw[:].bitcast(U16))
        deal(nc.vector.tensor_copy, wd_sc[:], wd_scales_raw[:])

        biased = {}
        h_words, h_scales, summed = {}, {}, {}

        def up(c, tag=""):
            lo, hi = CHUNKS[c]
            width = hi - lo
            h = [keep.tile([P, width * PACK], BF16, name="h%d_%d" % (c, g), tag="h%d_%d" % (c, g), align_bytes=64) for g in range(2)]
            h_words[c] = keep.tile([P, 2 * width], U32, name="h_words%d" % c, tag=tag, align_bytes=64)
            h_scales[c] = keep.tile([P, 2 * width], U8, name="h_scales%d" % c, align_bytes=64)
            for g in range(2):
                for j0 in range(0, width, P):
                    bank = up_banks.tile([P, PACK, P], F32, name="up_bank")
                    for t in range(PACK):
                        col = PASS * g + P * t
                        nc.tensor.matmul_mx(
                            out=bank[:, t, :],
                            lhsT=wu[:, 2 * col : 2 * (col + P)].bitcast(FP4X4),
                            lhsT_scale=wu_sc[:, col : col + P],
                            rhs=picked_words[c][:, j0 : j0 + P].bitcast(FP8X4),
                            rhs_scale=picked_scales[:, lo + j0 : lo + j0 + P],
                            start=True,
                            stop=True,
                        )
                    nc.scalar.activation(
                        out=h[g][:, PACK * j0 : PACK * (j0 + P)].rearrange("p (j t) -> p j t", t=PACK),
                        in_=bank[:].rearrange("p t j -> p j t"),
                        func=ACT.Relu,
                    )
                nc.vector.quantize_mx(
                    out=h_words[c][:, g * width : (g + 1) * width].bitcast(FP8X4),
                    scales=h_scales[c][:, g * width : (g + 1) * width],
                    in_=h[g][:],
                )

        def down(c, slots):
            lo, hi = CHUNKS[c]
            width = hi - lo
            for t in slots:
                bank = down_banks.tile([P, 512], F32, name="down_bank")
                nc.tensor.matmul_mx(
                    out=bank[:, 0:width],
                    lhsT=wd8[:, P * t : P * (t + 1)].bitcast(FP8X4),
                    lhsT_scale=wd_sc[:, P * t : P * (t + 1)],
                    rhs=h_words[c][:, 0:width].bitcast(FP8X4),
                    rhs_scale=h_scales[c][:, 0:width],
                    start=True,
                    stop=False,
                )
                nc.tensor.matmul_mx(
                    out=bank[:, 0:width],
                    lhsT=wd4[:, 2 * P * t : 2 * P * (t + 1)].bitcast(FP4X4),
                    lhsT_scale=wd_sc[:, N + P * t : N + P * (t + 1)],
                    rhs=h_words[c][:, width : 2 * width].bitcast(FP8X4),
                    rhs_scale=h_scales[c][:, width : 2 * width],
                    start=False,
                    stop=True,
                )
                if t < 2:
                    biased[t, lo] = keep.tile([P, width], F32, name="biased%d_%d" % (t, c), tag="biased%d_%d" % (t, c), align_bytes=64)[:]
                elif c == 0:
                    biased[t, lo] = keep.tile([P, J], F32, name="biased%d" % t, align_bytes=64)[:]
                nc.scalar.activation(
                    out=biased[t, lo] if t < 2 else biased[t, 0][:, lo:hi], in_=bank[:, 0:width], func=ACT.Identity, bias=bias[:, t : t + 1]
                )

        def add_residual(t, lo, hi, tag=""):
            summed[t, lo] = keep.tile([P, hi - lo], F32, name="summed%d_%d" % (t, lo), tag=tag, align_bytes=64)
            nc.vector.tensor_tensor(summed[t, lo][:], residual[t][:].indirect(entries(lo, hi)), biased[t, lo], ALU.add)

        def place(t, lo, hi):
            nc.vector.tensor_tensor(pages[t][:].indirect(entries(lo, hi)), summed[t, lo][:], weight[:, lo:hi], ALU.mult)

        n_out = len(OUT_CHUNKS)
        on_vector = ON_VECTOR
        widths = [hi - lo for lo, hi in OUT_CHUNKS]
        grouped = [keep.tile([P, widths[k], PACK], BF16, name="grouped%d" % k, align_bytes=64) for k in range(n_out)]
        pairs = [keep.tile([P, 2, widths[k]], BF16, name="pairs%d" % k, align_bytes=64) for k in range(on_vector)]
        out_words = keep.tile([P, T], U32, name="out_words", align_bytes=64)
        out_scales = keep.tile([P, T], U8, name="out_scales", align_bytes=64)

        def cols(k):
            return slice(*OUT_CHUNKS[k])

        def finish(t):
            nc.sync.dma_start(out=out_rows[t], in_=pages[t][:])
            if t < PACK - 1:
                for k in range(n_out):
                    if t == 2 and k < on_vector:
                        nc.scalar.copy(out=pairs[k][:, 0, :], in_=pages[t][:, cols(k)])
                    else:
                        nc.scalar.copy(out=grouped[k][:, :, t], in_=pages[t][:, cols(k)])

        up(0)
        down(0, (0, 1))
        pick_words(2, keep, tag="h0_1")
        add_residual(0, 0, 256)
        place(0, 0, 256)
        up(1, "biased0_0")
        down(1, (0, 1))
        add_residual(1, 0, 256, tag="h1_1")
        place(1, 0, 256)
        add_residual(0, 256, 512)
        place(0, 256, 512)
        up(2, "biased0_1")
        down(2, (0, 1))
        add_residual(1, 256, 512, tag="h2_1")
        place(1, 256, 512)
        add_residual(0, 512, J)
        add_residual(1, 512, J)
        for c in range(len(CHUNKS)):
            down(c, (2, 3))
        place(0, 512, J)
        finish(0)

        page2 = keep.tile([P, T], F32, name="page2", tag="residual0", align_bytes=64)
        page3 = keep.tile([P, T], F32, name="page3", tag="residual1", align_bytes=64)
        pages.extend([page2, page3])
        nc.gpsimd.memset(page2[:], 0.0)
        nc.gpsimd.memset(page3[:], 0.0)

        add_residual(2, 0, J)
        place(1, 512, J)
        finish(1)
        add_residual(3, 0, J)
        place(2, 0, J)
        finish(2)
        place(3, 0, J)
        finish(3)

        for k in range(on_vector, n_out):
            nc.scalar.copy(out=grouped[k][:, :, 3], in_=pages[3][:, cols(k)])
        for k in range(on_vector):
            nc.vector.tensor_copy(out=pairs[k][:, 1, :], in_=pages[3][:, cols(k)])
        for k in range(on_vector):
            nc.vector.tensor_copy(out=grouped[k][:, :, 2:4], in_=pairs[k][:].rearrange("p e c -> p c e"))
        words_out = out_1[0].rearrange("p c i -> p (c i)").bitcast(I32)
        stored = 0
        for k in range(n_out):
            nc.vector.quantize_mx(
                out=out_words[:, cols(k)].bitcast(FP8X4),
                scales=out_scales[:, cols(k)],
                in_=grouped[k][:].rearrange("p c t -> p (c t)"),
            )
            if k >= ON_VECTOR:
                done = slice(stored, OUT_CHUNKS[k][1])
                stored = OUT_CHUNKS[k][1]
                nc.sync.dma_start(out=words_out[:, done], in_=out_words[:, done].bitcast(I32))
        for q in range(4):
            queue = nc.sync if q % 2 else nc.scalar
            queue.dma_start(out=out_2[0][4 * q : 4 * q + 4, :].bitcast(I32), in_=out_scales[32 * q : 32 * q + 4, :].bitcast(I32))
